import numpy as np, ml_dtypes
CORES = [2,3,42,43,82,83,122,123]
N = 8
import mx_ref
BF = ml_dtypes.bfloat16
def entries(a):
    return np.ascontiguousarray(a.T).reshape(-1)
def table(e):
    return np.ascontiguousarray(np.reshape(e, (-1, 16)).T).astype(np.int32)
def gcols(t, e):
    v = np.concatenate([t.reshape(8, 16, -1, 4), np.zeros((8, 16, 1, 4), BF)], axis=2)
    return np.ascontiguousarray(np.stack([v[g][:, e[g]] for g in range(8)])).reshape(128, -1)
def cols(t, e):
    v = np.concatenate([t.reshape(128, -1, 4), np.zeros((128, 1, 4), BF)], axis=1)
    return np.ascontiguousarray(v[:, e]).reshape(128, -1)
def tile(rs):
    return np.stack(rs, axis=2).reshape(128, -1).astype(BF)
def cut(t, i, w=512):
    return t[:, w * i:w * i + w]
def pick(q, e):
    c = np.concatenate([q[0].reshape(128, -1, 4), np.zeros((128, 1, 4), np.uint8)], axis=1); s = np.concatenate([q[1], np.ones((16, 1), np.uint8)], axis=1)
    return (np.ascontiguousarray(c[:, e].reshape(128, -1)), np.ascontiguousarray(s[:, e]))
def join(*qs):
    return (np.concatenate([q[0] for q in qs], axis=1), np.concatenate([q[1] for q in qs], axis=1))
def put(q, e, v):
    c, s = q[0].reshape(128, -1, 4).copy(), q[1].copy(); c[:, e] = v[0].reshape(128, -1, 4); s[:, e] = v[1]
    return (c.reshape(128, -1), s)
def pk(c, s):
    return (np.ascontiguousarray(c), mx_ref.live(s))
def emit(q):
    return q[0], q[1]
def packed(v, rng):
    q = [mx_ref.quantize(np.ascontiguousarray(v[r])) for r in range(N)]
    return np.stack([a for a, b in q]), np.stack([mx_ref.plane(b, rng) for a, b in q])
def values_of_codes():
    e, c = np.zeros((128, 128, 4), np.float32), np.zeros((128, 2, 4), np.uint8)
    e[np.arange(128), np.arange(128), 0] = 1
    c[:127, :, 0] = np.arange(256).reshape(2, 128).T[:127]
    return mx_ref.matmul(mx_ref.quantize(e.reshape(128, 512).astype(BF)), (c.reshape(128, 8), np.full((16, 2), 127, np.uint8))).T.reshape(-1).astype(np.float64)
CODE_VALUE, SCALE_VALUE = values_of_codes(), 2.0 ** (np.arange(256) - 127.0)
def decode(q):
    return (CODE_VALUE[q[0]].reshape(16, 8, -1, 4) * SCALE_VALUE[q[1]][:, None, :, None] + 0.0).reshape(128, -1).astype(np.float32)
def f(rng, *shape):
    return mx_ref.flush((rng.standard_normal(shape, dtype=np.float32) * np.exp2(rng.integers(-2, 3, shape[:-1] + (1,)))).astype(BF))
def wide(rng, *shape, cols=0):
    v = rng.standard_normal(shape, dtype=np.float32) * np.exp2(rng.integers(-12, 13, shape)).astype(np.float32)
    if cols: v *= np.repeat(np.exp2(rng.integers(-cols, cols + 1, shape[:-2] + (1, shape[-1] // 4))) * (rng.random(shape[:-2] + (1, shape[-1] // 4)) > 0.0625), 4, axis=-1).astype(np.float32)
    return mx_ref.flush(v.astype(BF))
C, M, F, R = 384, 96, 4, 3
def order(p):
    return np.argsort(-(p[::16] + np.float32(0.0)), axis=1, kind="stable")
def rewrite(t, e, h):
    a, b = t.reshape(8, 16, -1, 4).copy(), h.reshape(8, 16, -1, 4)
    for g in range(8):
        c, j = np.unique(e[g], return_index=True)
        a[g][:, c] = b[g][:, j]
    return a.reshape(128, -1)
def big(v):
    v = v.astype(np.float32)
    v[np.abs(v) < np.float32(2.0 ** -16)] = 0
    return v.astype(BF)
def offsets(a):
    return np.stack([table(np.concatenate([k, np.full(16 - F, -1)])) for k in a])
def numbers_of(rng):
    return {"x": big(f(rng, N, 128, 4 * C)), "m": big(f(rng, N, 128, 4 * M)), "kap": offsets(rng.integers(0, C, (N, F))), "u": np.array(f(rng, N, 128, 512)), "v": np.array(f(rng, N, 128, 512))}
def layers(rng):
    return big(f(rng, N, 128, 2048)).reshape(N, 8, 16, 4, 8, 16, 4)
def weights(rng, w):
    c, p = packed(np.ascontiguousarray(w).reshape(N, 128, 2048), rng)
    return {"wc": c, "ws": p}
def setup_inputs(rng):
    return {**numbers_of(rng), **weights(rng, layers(rng))}
def setup_inputs_ties(rng):
    d = numbers_of(rng)
    e = rng.permutation(N)
    x, m = d["x"].reshape(N, 8, 16, C, 4), d["m"].reshape(N, 8, 16, M, 4)
    for r in range(N):
        k = np.zeros(C, int) if r == e[0] else rng.permutation(C) % 3
        i = np.zeros(M, int) if r == e[0] else rng.permutation(M) % 3
        a = x[r][:, :8, :3].copy()
        a[:, :, 2] = 0
        x[r][:, :8] = a[:, :, k]
        m[r][:, :8] = a[:, :, i]
    x[e[1]] = 0
    u = d["u"].reshape(N, 8, 16, 128, 4)
    u[:, :, 8:, ::16] = 0
    u[:, :, 8:, 1] = 0
    w = layers(rng)
    w[:, :, 8:, :, :, :8] = 0
    kap = offsets(rng.integers(0, C, (N, 2))[:, rng.permutation(4) % 2])
    return {"x": x.reshape(N, 128, 4 * C), "m": m.reshape(N, 128, 4 * M), "kap": kap, "u": u.reshape(N, 128, 512), "v": d["v"], **weights(rng, w)}
def near_part(rng, s, b, size):
    p = np.zeros((16, s.size, 4))
    p[0, :, 0] = b
    g = ((s[:, None] >> np.arange(8)) & 1) * np.exp2(np.arange(8) - 23.0) * size
    p[8], p[9] = g[:, :4], g[:, 4:]
    p[10:] = rng.integers(4, 8, (6, s.size, 4)) * 2.0 ** -20 * size
    return p
def setup_inputs_near(rng):
    d = numbers_of(rng)
    kind = rng.permutation(8)
    c = np.where(kind < 6, kind % 2 * 2.0 - 1.0, 0.0)
    x, m = np.zeros((N, 8, 16, C, 4), np.float32), np.zeros((N, 8, 16, M, 4), np.float32)
    upper = np.arange(C) // (C // 2)
    for r in range(N):
        for g in range(8):
            i = (np.arange(C) + rng.integers(C)) % C
            b, a = np.full(C, c[g]), np.full(M, c[g])
            if kind[g] < 4: b[rng.integers(C)] *= 2.0 ** 30
            if kind[g] == 7:
                i = i % (C // 2) * 2 + upper
                b, a = (8 + upper) * 2.0 ** -33, (8 + rng.integers(0, 2, M)) * 2.0 ** -33
            size = 1.0 if kind[g] < 6 else 2.0 ** -4
            x[r, g] = near_part(rng, (i + 1) // 2, b, size)
            m[r, g] = near_part(rng, rng.integers(0, C // 2 + 1, M), a, size)
            if kind[g] == 7:
                x[r, g, 1, :, 0] = 17 * 2.0 ** -33 - b
                m[r, g, 1, :, 0] = 17 * 2.0 ** -33 - a
    u = d["u"].reshape(N, 128, 128, 4)
    k = np.where(rng.permutation(N) < N // 2, 2.0 ** -30, 1.0).astype(np.float32).astype(BF)
    u[:, :, ::16] = 0
    u[:, :, 1] = 0
    for h in range(0, 128, 16):
        u[:, h, h, 0] = k
        u[:, h + 8:h + 10, h] = k[:, None, None]
    h = 16 * int(np.argmax(kind))
    u[:, h, h, 0] = (k.astype(np.float32) * np.float32(1.125)).astype(BF)
    u[:, h + 1, h, 0] = k
    sort = rng.permutation(np.array([0, 5, 6, 7, 1, 2, 3, 4])[:N])
    one = np.argsort(kind)[sort]
    a = rng.integers(0, C, (N, F))
    for r in range(N):
        h = 16 * int(one[r])
        u[r, h:h + 16, 1] = u[r, h:h + 16, h]
        if sort[r] in (0, 5, 6, 7): a[r] = np.insert(rng.permutation(3), int(rng.integers(1, 4)), C - 1)
    w = layers(rng)
    w[:, :, :10] = 0
    w[:, :, :, :, :, :10] = 0
    w[:, :, :, :, np.flatnonzero(kind > 5)] = 0
    return {"x": x.reshape(N, 128, 4 * C).astype(BF), "m": m.reshape(N, 128, 4 * M).astype(BF), "kap": offsets(a), "u": u.reshape(N, 128, 512), "v": d["v"], **weights(rng, w)}
def setup_inputs_huge(rng):
    d = numbers_of(rng)
    o = rng.permutation(N)
    t = {}
    for key, n in (("x", C), ("m", M)):
        c = np.stack([rng.permutation(n) % 2 * 2.0 - 1.0 for r in range(N)])
        c[o < N // 2] = -1
        z = rng.random((N, 128, n, 4))
        z[:, ::8, :, 0] = 0
        t[key] = np.where(c[:, None, :, None] < 0, -2.0 ** 30 * (1 - 0.125 * z), 2.0 ** 28 * (0.8 - 0.2 * z)).astype(np.float32).reshape(N, 128, 4 * n).astype(BF)
    u = d["u"].reshape(N, 128, 128, 4)
    s = np.stack([np.append(rng.permutation(8) % 2 * 2.0 - 1.0, o[r] % 2 * 2.0 - 1.0) for r in range(N)])
    a = (2.0 ** 30 * (1 - 0.0625 * rng.integers(0, 2, (N, 128, 9, 4))) * s[:, None, :, None]).astype(np.float32).astype(BF)
    u[:, :, ::16] = a[:, :, :8]
    u[:, :, 1] = a[:, :, 8]
    w = np.zeros((N, 128, 4, 128, 4), np.float32)
    i = np.arange(128)
    for b in range(4): w[:, i, b, i, b] = 16
    return {"x": t["x"], "m": t["m"], "kap": d["kap"], "u": u.reshape(N, 128, 512), "v": d["v"], **weights(rng, w.astype(BF))}
def setup_inputs_wrap(rng):
    d = numbers_of(rng)
    x, m = d["x"].astype(np.float32).reshape(N, 8, 16, C, 4), d["m"].astype(np.float32).reshape(N, 8, 16, M, 4)
    u = d["u"].reshape(N, 128, 128, 4)
    x[:, :, :11] = 0
    m[:, :, :11] = 0
    u[:, :, ::16] = 0
    u[:, :, 1] = 0
    a = np.stack([rng.permutation(np.array([0, 1, C // 2, C - 1])) for r in range(N)])
    a[rng.integers(N)] = C - 1
    q = rng.integers(0, C + 1, (N, 8, M))
    o = rng.permutation(N)
    for r in range(N):
        g = rng.permutation(8)
        q[r, g[0]] = 0
        q[r, g[1]] = C
        q[r, g[2]] = rng.permutation(C)[:M]
        q[r, g[3]] = rng.integers(C - 2, C + 1, M)
        q[r, g[4]] = (rng.integers(C) - a[r][rng.integers(0, F, M)]) % C
        x[r, g[2], 0, :, 0] = rng.integers(1, 8, C)
        m[r, g[2], 0, :, 0] = rng.integers(1, 8, M)
        u[r, 16 * g[2], 1, 0] = -1 if o[r] < N // 2 else 1
    for h in range(0, 128, 16): u[:, h + 8:h + 11, h] = 1
    for t, key in ((x, 2 * (C - np.argsort(rng.random((N, 8, C)), axis=2))), (m, 2 * (C - q) + rng.integers(0, 2, q.shape))):
        z = ((key[:, :, :, None] >> np.arange(12)) & 1) * np.exp2(np.arange(12.0))
        for i in range(3): t[:, :, 8 + i] = z[:, :, :, 4 * i:4 * i + 4]
    w = layers(rng)
    w[:, :, :11] = 0
    w[:, :, :, :, :, :11] = 0
    return {"x": x.reshape(N, 128, 4 * C).astype(BF), "m": m.reshape(N, 128, 4 * M).astype(BF), "kap": offsets(a), "u": u.reshape(N, 128, 512), "v": d["v"], **weights(rng, w)}
def setup_inputs_spread(rng):
    d = setup_inputs(rng)
    d["x"] = big(wide(rng, N, 128, 4 * C, cols=6))
    d["m"] = big(wide(rng, N, 128, 4 * M, cols=6))
    return d
def check_inputs(d):
    b = []
    for k in ("x", "m", "u", "v"):
        a = np.abs(d[k].astype(np.float32))
        if not (np.isfinite(a).all() and ((a == 0) | (a >= 2.0 ** -30) & (a <= 2.0 ** 30)).all()): b.append("a value of " + k)
    none, least, most = [emit(mx_ref.quantize(np.full((128, 16), k, np.float32).astype(BF)))[1][0, 0] for k in (0.0, 2.0 ** -30, 2.0 ** 30)]
    for r in range(N):
        k = entries(d["kap"][r])
        if ((k[:F] < 0) | (k[:F] >= C)).any(): b.append("an offset of kap")
        if (k[F:] != -1).any(): b.append("kap: an entry that means nothing isn't -1")
        if ((d["wc"][r] == 0x7F) | (d["wc"][r] == 0xFF)).any(): b.append("wc: a code that is no number")
        s = mx_ref.live(d["ws"][r])
        if ((s != none) & ((s < least) | (s > most))).any(): b.append("ws: a scale out of range")
    return b
def reference(x, m, kap, u, v, wc, ws):
    qu = [mx_ref.quantize(u[r]) for r in range(N)]
    lay = [pk(wc[r], ws[r]) for r in range(N)]
    disc, msg = [x[r] for r in range(N)], [m[r] for r in range(N)]
    ok = np.zeros((N, R, M), np.float32)
    for t in range(R):
        won = []
        for r in range(N):
            p = mx_ref.matmul(qu[r], mx_ref.quantize(disc[r]))
            s = mx_ref.matmul(qu[r], mx_ref.quantize(msg[r]))
            n = np.sum(p[::16][:, :, None] > s[::16][:, None, :], axis=1)
            c = (n[:, None, :] + entries(kap[r])[:F][None, :, None]) % C
            e = np.take_along_axis(order(p), c.reshape(8, F * M), axis=1)
            z = ((gcols(disc[r], e).astype(np.float32) + np.tile(msg[r], (1, F)).astype(np.float32)) * np.float32(0.5)).astype(BF)
            best = np.argmax(mx_ref.matmul(qu[r], mx_ref.quantize(z))[1].reshape(F, M) + np.float32(0.0), axis=0)
            i = best * M + np.arange(M)
            h = cols(z, i)
            disc[r] = rewrite(disc[r], e[:, i], h)
            ok[r, t] = best
            won.append(mx_ref.quantize(h))
        came = decode(join(*won))
        for r in range(N):
            o = (r - 1) % N
            n = cut(came, o, 4 * M)
            msg[r] = tile([np.maximum(mx_ref.matmul(pick(lay[r], np.arange(128 * b, 128 * b + 128)), won[o]), np.float32(0.0)) * np.float32(0.03125) + n[:, b::4] for b in range(4)])
    y = np.zeros((N, 128, C + M), np.float32)
    oc, osc = np.zeros((N, 128, 4 * C + 4 * M), np.uint8), np.zeros((N, 16, C + M), np.uint8)
    for r in range(N):
        q = mx_ref.quantize(np.concatenate([disc[r], msg[r]], axis=1))
        y[r] = mx_ref.matmul(mx_ref.quantize(v[r]), q)
        oc[r], osc[r] = emit(q)
    return {"y": y, "ok": ok, "oc": oc, "osc": osc}

@@ -1,0 +1,465 @@
+from concourse.mybir import dt, AluOpType as ALU, ActivationFunctionType as ACT
+
+C, M, R = 384, 96, 3
+BIG = 2.0 ** 98
+K = 16384.0
+NV = 10
+TW = [384, 320, 256, 192, 128, 128]
+TO = [0, 384, 704, 960, 1152, 1280]
+MO = [0, 96, 192, 320, 416, 512]
+CODES = "float8_e4m3fn_x4"
+
+SCRATCH = {"ps": ("psum", [128, 4096], "float32")}
+for _n, _w in (("X", 1920), ("Y", 512), ("Xh", 1536), ("Yh", 384), ("Z", 1536), ("Hp", 384), ("ut", 512), ("vt", 512),
+               ("MT", 4 * 1408), ("MM", 4 * 640), ("junk", 4416), ("ones", 512), ("blk0", 512), ("blk", 512),
+               ("Et", 2048), ("zero", 512), ("cm16", 384), ("Bm", 384), ("Am", 384), ("Rst", 384), ("Cc", 384),
+               ("C4", 288), ("cdv", 576), ("Cd", 576), ("EQ", 576), ("ds", 576), ("drow", 384)):
+    SCRATCH[_n] = ("sbuf", [128, _w], "bfloat16")
+for _n, _w in (("col", 16), ("i16", 24), ("JJ", 24), ("Ctab", 24), ("DUM", 6), ("V16", 48), ("V4", 12), ("kf", 16),
+               ("kb", 16), ("cvals", 384), ("msk", 384), ("Sc", 384), ("Rtab", 24), ("CD", 24), ("CR", 24),
+               ("CRK", 24), ("nst", 96), ("pos", 24), ("pwr", 24), ("pos2", 24), ("pst", 384), ("pl", 24), ("O", 384),
+               ("E", 384), ("Tst", 384), ("sm", 384), ("ss", 384), ("Mx", 18), ("G", 18), ("hh", 6), ("GJ", 18),
+               ("AB", 18), ("Bh", 6), ("IDX", 18), ("wrow", 96), ("wm", 96), ("wS", 96), ("zz", 6), ("w2", 6),
+               ("RL", 384), ("kd", 32), ("kk", 32), ("kT", 32), ("yo", 480)):
+    SCRATCH[_n] = ("sbuf", [128, _w], "float32")
+for _n, _w in (("pi", 2), ("pj", 4), ("uli", 16), ("ki", 16)):
+    SCRATCH[_n] = ("sbuf", [128, _w], "int32")
+for _n, _w in (("ul", 16), ("Lp", 24), ("Lpos", 24), ("LT", 96), ("L96", 6), ("LH", 24), ("LS", 24)):
+    SCRATCH[_n] = ("sbuf", [128, _w], "uint16")
+for _n, _w in ([("u0", 128), ("ub", 256), ("v0", 128), ("w0", 512), ("e0", 512), ("one", 128), ("a", 512),
+                ("mt", 1408), ("mm", 640)] + [("z%d" % _t, 384) for _t in range(R)]
+               + [("h%d" % _t, 96) for _t in range(R)] + [("l%d" % _t, 224) for _t in range(R)]):
+    SCRATCH["q" + _n] = ("sbuf", [128, _w], CODES)
+    SCRATCH["s" + _n] = ("sbuf", [128, _w], "uint8")
+
+SEMAPHORES = ["sv", "sa", "st", "sg", "sent", "arr0", "arr1", "arr2"] + ["d%d" % _i for _i in range(24)]
+
+
+def rank_program(g, core, T, topo):
+    rank = T.rank_of(core)
+    if rank is None:
+        return
+    n = len(T.cores)
+    nxt, prv = T.cores[(rank + 1) % n], T.cores[(rank - 1) % n]
+    Q = {"v": g.vector, "a": g.scalar, "t": g.tensor, "g": g, "s": g.sync}
+    SEM = {"v": "sv", "a": "sa", "t": "st", "g": "sg"}
+    count = {"v": 0, "a": 0, "t": 0, "g": 0, "d": 0, "sent": 0, "all": 0}
+    known = {q: {} for q in Q}
+    hist = {}
+    last = {}
+
+    def V(name, a=0, b=None, s=1, p=None):
+        if b is None:
+            b = SCRATCH[name][1][1]
+        m = 0
+        if s == 1:
+            m = ((1 << (b - a)) - 1) << a
+        else:
+            for i in range(a, b, s):
+                m |= 1 << i
+        rows = slice(0, 128) if p is None else slice(p[0], p[1])
+        ap = T[name][rows, a:b] if s == 1 else T[name][rows, a:b:s]
+        return (ap, name, m)
+
+    def PS(bank, a, b):
+        return (T.ps[:, 512 * bank + a:512 * bank + b], "ps%d" % bank, 1)
+
+    def need(q, reads, writes):
+        deps = []
+        for vs, w in ((reads, False), (writes, True)):
+            for x in vs:
+                bank = x[1].startswith("ps")
+                for (m, w2, tok, q2) in hist.get(x[1], []):
+                    if m & x[2] and (w or w2 or (bank and q2 != q)) and not (q == "t" and q2 == "t"):
+                        deps.append(tok)
+        deps.sort(key=lambda k: -k[3])
+        for sem, val, clock, _ in deps:
+            if known[q].get(sem, 0) < val:
+                Q[q].wait_ge(T.sem[sem], val)
+                known[q][sem] = val
+                for s2, v2 in clock.items():
+                    if known[q].get(s2, 0) < v2:
+                        known[q][s2] = v2
+
+    def note(q, sem, val, reads, writes):
+        count["all"] += 1
+        tok = (sem, val, dict(known[q]) if q in known else {}, count["all"])
+        last[sem] = val
+        for vs, w in ((reads, False), (writes, True)):
+            for x in vs:
+                h = hist.setdefault(x[1], [])
+                if w:
+                    h[:] = [e for e in h if e[0] & ~x[2]]
+                h.append((x[2], w, tok, q))
+
+    def op(q, fn, reads, writes):
+        reads = [x for x in reads if isinstance(x, tuple)]
+        need(q, reads, writes)
+        count[q] += 1
+        fn().then_inc(T.sem[SEM[q]], 1)
+        note(q, SEM[q], count[q], reads, writes)
+
+    def dma(q, out, in_, reads, writes):
+        need(q, reads, writes)
+        sem = "d%d" % count["d"]
+        count["d"] += 1
+        Q[q].dma_start(out, in_).then_inc(T.sem[sem], 16)
+        note(q, sem, 16, reads, writes)
+
+    def A(x):
+        return x[0] if isinstance(x, tuple) else x
+
+    def tt(out, a, b, o, off=None):
+        i0 = a[0] if off is None else a[0].indirect(off[0])
+        op("v", lambda: g.vector.tensor_tensor(out[0], i0, b[0], o), [a, b, off], [out])
+
+    def ts(out, a, s1, o0, s2=None, o1=None):
+        if o1 is None:
+            op("v", lambda: g.vector.tensor_scalar(out[0], a[0], A(s1), None, o0), [a, s1], [out])
+        else:
+            op("v", lambda: g.vector.tensor_scalar(out[0], a[0], A(s1), A(s2), o0, o1), [a, s1, s2], [out])
+
+    def cp(out, a):
+        op("v", lambda: g.vector.tensor_copy(out[0], a[0]), [a], [out])
+
+    def gather(out, win, off):
+        op("v", lambda: g.vector.tensor_copy(out[0], win[0].indirect(off[0])), [win, off], [out])
+
+    def scatter(win, off, a):
+        op("v", lambda: g.vector.tensor_copy(win[0].indirect(off[0]), a[0]), [a, off], [win])
+
+    def scan(out, d0, d1, init, o0, o1):
+        op("v", lambda: g.vector.tensor_tensor_scan(out[0], d0[0], d1[0], init, o0, o1), [d0, d1], [out])
+
+    def fill(out, c):
+        op("v", lambda: g.vector.memset(out[0], c), [], [out])
+
+    def act(out, a, f, bias=None, scale=None, acc=None, off=None):
+        kw = {}
+        if bias is not None:
+            kw["bias"] = A(bias)
+        if scale is not None:
+            kw["scale"] = A(scale)
+        if acc is not None:
+            kw["accum_out"] = acc[0]
+        i0 = a[0] if off is None else a[0].indirect(off[0])
+        op("a", lambda: g.scalar.activation(out[0], i0, f, **kw), [a, bias, scale, off],
+           [out] + ([acc] if acc is not None else []))
+
+    def quant(name, c0, tile, t0, cols):
+        o, s, i = V("q" + name, c0, c0 + cols), V("s" + name, c0, c0 + cols), V(tile, 4 * t0, 4 * (t0 + cols))
+        op("v", lambda: g.vector.quantize_mx(o[0], s[0], i[0]), [i], [o, s])
+
+    def mm(bank, w, w0, x, x0, cols, start=True, stop=True):
+        o = PS(bank, 0, cols)
+        a, sa = V("q" + w, w0, w0 + 128), V("s" + w, w0, w0 + 128)
+        b, sb = V("q" + x, x0, x0 + cols), V("s" + x, x0, x0 + cols)
+        op("t", lambda: g.tensor.matmul_mx(o[0], a[0], sa[0], b[0], sb[0], start, stop), [a, sa, b, sb], [o])
+
+    def pick_codes(dst, src, width, off):
+        o, w = V("q" + dst), V("q" + src, 0, width)
+        op("v", lambda: g.vector.tensor_copy(o[0].bitcast(dt.uint32), w[0].bitcast(dt.uint32).indirect(off[0])),
+           [w, off], [o])
+
+    def pick_scales(dst, src, width, off):
+        act(V("s" + dst), V("s" + src, 0, width), ACT.Copy, off=off)
+
+    def iota(out, pattern, base, cm, whole=False):
+        if whole:
+            op("g", lambda: g.iota(out[0], pattern, base, cm), [], [out])
+        else:
+            op("g", lambda: g.iota(out[0], pattern, base, cm, allow_small_or_imprecise_dtypes=True), [], [out])
+
+    def zeros(name, a, b):
+        iota(V(name, a, b), [[0, b - a]], 0, 0)
+
+    def select(out, a, pattern, cmp, base, cm):
+        op("g", lambda: g.affine_select(out[0], a[0], pattern, cmp, 0.0, base, cm), [a], [out])
+
+    def col(i):
+        return V("col", i, i + 1)
+
+    eng_in = len(topo.engines(prv, core))
+    for t in range(R):
+        note("remote", "arr%d" % t, 2 * eng_in, [], [V("ql%d" % t, 0, M), V("sl%d" % t, 0, M)])
+
+    dma("a", V("ut")[0], T.u[:], [], [V("ut")])
+    dma("s", V("X", 1024, 1536)[0], T.x[:, 1024:1536], [], [V("X", 1024, 1536)])
+    dma("s", V("X", 0, 1024)[0], T.x[:, 0:1024], [], [V("X", 0, 1024)])
+    dma("s", V("Y", 0, 384)[0], T.m[:], [V("X", 1024, 1536)], [V("Y", 0, 384)])
+    dma("s", V("ki", p=(0, 1))[0], T.kap[:], [], [V("ki")])
+    dma("s", T.qw0[:].bitcast(dt.uint8), T.wc[:], [V("Y", 0, 384)], [V("qw0")])
+    dma("s", T.sw0[:], T.ws[:], [], [V("sw0")])
+    dma("s", V("vt")[0], T.v[:], [], [V("vt")])
+
+    cR, cA, cT, cR1, cA1, cS16, cK16, cS4, cT4, cNR = range(10)
+    iota(V("pi"), [[0, 2]], 0, 1, whole=True)
+    iota(V("uli", 0, 8), [[16, 8]], 0, 0, whole=True)
+    iota(V("cm16"), [[0, 24], [1, 16]], 0, 0)
+    iota(V("i16"), [[16, 24]], 0, 0)
+    fill(V("uli", 8, 16), 1)
+    fill(V("ones"), 1.0)
+    ts(V("pj", 0, 1), V("pi", 0, 1), 15, ALU.bitwise_and)
+    ts(V("pj", 1, 2), V("pi", 0, 1), 2, ALU.logical_shift_right, 3, ALU.bitwise_and)
+    ts(V("pj", 2, 3), V("pi", 0, 1), 3, ALU.bitwise_and)
+    cp(V("ul"), V("uli"))
+    cp(V("col", 0, 3), V("pj", 0, 3))
+    fill(V("MT", 4 * (TO[5] + 16), 4 * 1408), 0.0)
+    ts(V("col", cR1, cA1 + 1), V("col", cR, cA + 1), 1.0, ALU.add)
+    ts(col(cS16), col(cR), 15.0, ALU.is_equal, 1.0 / K, ALU.max)
+    ts(col(cK16), col(cR), 15.0, ALU.not_equal, K, ALU.mult)
+    ts(col(cS4), col(cA), 3.0, ALU.is_equal, 1.0 / K, ALU.max)
+    ts(V("Bm"), V("cm16"), col(cR), ALU.not_equal, -BIG, ALU.mult)
+    ts(V("Am"), V("cm16"), 0.0, ALU.is_equal, -BIG, ALU.mult)
+    ts(V("V16", 0, 16), V("cm16", 0, 16), col(cR1), ALU.is_gt)
+    ts(V("V16", 16, 32), V("cm16", 0, 16), col(cR1), ALU.is_equal, K, ALU.mult)
+    ts(col(cT4), col(cT), -128.0, ALU.add)
+    tt(V("V16", 32, 48), V("V16", 0, 16), V("V16", 16, 32), ALU.add)
+    quant("u0", 0, "ut", 0, 128)
+    ts(col(cNR), col(cR), -1.0, ALU.mult)
+    pick_codes("ub", "u0", 128, V("ul"))
+    pick_scales("ub", "u0", 128, V("ul"))
+    for a in range(5):
+        zeros("MT", 4 * (TO[a] + TW[a] - 48), 4 * (TO[a] + TW[a]))
+    zeros("Y", 384, 512)
+    select(V("blk0"), V("ones"), [[-16, 8], [0, 64]], ALU.is_ge, 0, 1)
+    select(V("blk"), V("blk0"), [[16, 8], [0, 64]], ALU.is_ge, 15, -1)
+    zeros("MM", 4 * 288, 4 * 320)
+    zeros("MM", 4 * 608, 4 * 640)
+    zeros("Rtab", 0, 1)
+
+    def late_constants(part):
+        if part == 0:
+            ts(V("Rst"), V("cm16"), 0.0, ALU.not_equal)
+            ts(V("V4", 0, 4), V("cm16", 0, 4), col(cA1), ALU.is_gt)
+            ts(V("V4", 4, 8), V("cm16", 0, 4), col(cA1), ALU.is_equal, K, ALU.mult)
+            ts(V("JJ"), V("i16"), col(cR), ALU.add)
+            return
+        ts(V("Ctab"), V("i16"), col(cR), ALU.subtract, 15.0, ALU.add)
+        cp(V("kf", p=(0, 1)), V("ki", p=(0, 1)))
+        ts(col(cK16), col(cK16), 1.0, ALU.max)
+        ts(col(cS4), col(cS4), 4.0, ALU.mult)
+        tt(V("V4", 8, 12), V("V4", 0, 4), V("V4", 4, 8), ALU.add)
+        ts(V("DUM"), V("JJ", 0, 6), 416.0, ALU.add)
+        op("g", lambda: g.partition_broadcast(T.kb[:], T.kf[0:1, :], 128), [V("kf")], [V("kb")])
+        iota(V("cvals"), [[1, 384]], 32, 0)
+        zeros("O", 0, 384)
+        iota(V("cdv"), [[-16, 6], [1, 96]], 0, 0)
+        zeros("EQ", 0, 576)
+        zeros("zero", 0, 512)
+        zeros("kd", 0, 32)
+        for b in range(4):
+            select(V("Et", 512 * b, 512 * b + 512), V("ones"), [[1, 512]], ALU.is_equal, -b, -4)
+
+    def slot(i, a=0, b=None):
+        k, e = divmod(24 - i, 4)
+        b = 16 * i if b is None else b
+        return V("MT", 4 * (TO[k] + a) + e, 4 * (TO[k] + b), 4)
+
+    def pt(i):
+        return V("Sc", 16 * i + 15, 16 * i + 16)
+
+    def layer(t):
+        for b in range(4):
+            mm(4 + b, "w0", 128 * b, "l%d" % t, 0, 128)
+
+    def relu_then_d(t):
+        for b in range(4):
+            ts(V("RL", 96 * b, 96 * b + 96), PS(4 + b, 0, M), 0.0, ALU.max, 0.03125, ALU.mult)
+            mm(4 + b, "e0", 128 * b, "l%d" % t, 0, 128)
+
+    def add_d(bank0):
+        for b in range(4):
+            tt(V("Y", b, 384, 4), PS(bank0 + b, 0, M), V("RL", 96 * b, 96 * b + 96), ALU.add)
+
+    def disc_list(a, b):
+        scan(V("Tst", a, b), V("C4", 0, b - a), V("E", a, b), 0.0, ALU.mult, ALU.add)
+        ts(V("LT", a // 4, b // 4), V("Tst", a + 3, b, 4), col(cS4), ALU.mult, col(cT4), ALU.add)
+
+    for t in range(R):
+        quant("a", 256, "X", 256, 128)
+        mm(3, "ub", 0, "a", 256, 128)
+        if t == 0:
+            late_constants(0)
+            for c in range(16):
+                act(V("Cc", c, 384, 16), V("cm16", 0, 24), ACT.Identity, bias=V("V16", 32 + c, 33 + c), scale=0.0)
+        quant("a", 0, "X", 0, 256)
+        mm(1, "ub", 0, "a", 0, C)
+        mm(0, "ub", 0, "a", 0, 256)
+        if t > 0:
+            layer(t - 1)
+        tt(V("msk", 256, C), PS(3, 0, 128), V("Bm", 0, 128), ALU.add)
+        if t == 1:
+            quant("l1", M, "zero", 0, 128)
+        if t == 2:
+            quant("l2", M, "zero", 0, 128)
+        scan(V("Sc", 256, C), V("Am", 0, 128), V("msk", 256, C), -BIG, ALU.add, ALU.max)
+        if t == 0:
+            late_constants(1)
+        if t == 2:
+            quant("v0", 0, "vt", 0, 128)
+        tt(slot(24, 256, C), V("Sc", 256, C), PS(3, 0, 128), ALU.is_ge)
+        rows = list(range(23, NV, -1))
+        done = {}
+
+        def scalar_rows(upto):
+            while rows and rows[0] >= upto:
+                two = rows[:2]
+                del rows[:2]
+                for i in two:
+                    act(slot(i), PS(1, 0, 16 * i), ACT.Sign, bias=pt(i), scale=-1.0)
+                for i in two:
+                    act(slot(i), slot(i), ACT.Relu, acc=V("Rtab", i, i + 1))
+
+        def tile_sum(k, cols=None):
+            quant("mt", TO[k], "MT", TO[k], TW[k] if cols is None else cols)
+
+        def tile_mm(k):
+            done[k] = True
+            mm(2, "one", 0, "mt", TO[k], TW[k], len(done) == 1, len(done) == 6)
+
+        scalar_rows(17)
+        tt(V("msk", 0, 256), PS(0, 0, 256), V("Bm", 0, 256), ALU.add)
+        scan(V("Sc", 0, 256), V("Am", 0, 256), V("msk", 0, 256), -BIG, ALU.add, ALU.max)
+        tt(slot(24, 0, 256), V("Sc", 0, 256), PS(0, 0, 256), ALU.is_ge)
+        for i in range(NV, 0, -1):
+            ts(slot(i), PS(0, 0, 16 * i), pt(i), ALU.is_lt)
+        scan(V("drow"), V("Rst"), slot(24, 0, C), 0.0, ALU.mult, ALU.add)
+        if t > 0:
+            relu_then_d(t - 1)
+        tile_sum(0)
+        tt(V("CD"), V("Ctab"), V("drow", 15, 384, 16), ALU.subtract)
+        if t > 0:
+            add_d(4)
+        quant("a", C, "Y", 0, 128)
+        mm(3, "ub", 0, "a", C, 128)
+        if t == 0:
+            quant("one", 0, "blk", 0, 128)
+        tile_sum(4, 256 if t == 0 else 192)
+        tile_mm(0)
+        tile_mm(4)
+        tile_mm(5)
+        scalar_rows(1)
+        off = 0
+        for i in range(NV, 0, -1):
+            act(V("junk", off, off + 16 * i), slot(i), ACT.Identity, acc=V("Rtab", i, i + 1))
+            off += 16 * i
+        for half in range(2):
+            for i in range(12 * half, 12 * half + 12):
+                k, e = divmod(i, 4)
+                ts(V("MM", 4 * MO[k] + e, 4 * (MO[k] + M), 4), PS(3, 0, M), pt(i), ALU.is_lt)
+                if i % 12 == 5:
+                    tile_sum(1 + half)
+                    tile_mm(1 + half)
+            quant("mm", 320 * half, "MM", 320 * half, 320 if t == 0 else 288)
+            for k in range(3 * half, 3 * half + 3):
+                mm(4, "one", 0, "mm", MO[k], 128, k == 0, k == 5)
+        tile_sum(3)
+        tile_mm(3)
+        tt(V("CR"), V("CD"), V("Rtab"), ALU.subtract)
+        scan(V("nst"), V("Cc", 0, M), PS(4, 0, M), 0.0, ALU.mult, ALU.add)
+        ts(V("CRK"), V("CR"), col(cK16), ALU.mult)
+        for k in range(4):
+            act(V("pos", 6 * k, 6 * k + 6), V("nst", 15, M, 16), ACT.Identity, bias=V("kb", k, k + 1), scale=col(cS16))
+        scan(V("pst"), V("Cc"), PS(2, 0, C), 0.0, ALU.mult, ALU.add)
+        tt(V("pl"), V("pst", 15, C, 16), V("CRK"), ALU.add)
+        ts(V("pwr"), V("pos"), float(C), ALU.is_ge, -float(C), ALU.mult)
+        ts(V("Lp"), V("pl"), col(cS16), ALU.mult)
+        tt(V("pos2"), V("pos"), V("pwr"), ALU.add)
+        if t == 0:
+            for c in range(4):
+                act(V("C4", c, 288, 4), V("cm16", 0, 72), ACT.Identity, bias=V("V4", 8 + c, 9 + c), scale=0.0)
+        act(V("Xh"), V("X", 0, 1536), ACT.Identity, scale=0.5)
+        act(V("Yh"), V("Y", 0, 384), ACT.Identity, scale=0.5)
+        cp(V("Lpos"), V("pos2"))
+        scatter(V("O"), V("Lp"), V("cvals"))
+        act(V("E", M, C), V("O"), ACT.Copy, off=V("Lpos", 6, 24))
+        gather(V("E", 0, M), V("O"), V("Lpos", 0, 6))
+        disc_list(0, M)
+        if t == 0:
+            act(V("Cd"), V("cdv"), ACT.Abs, bias=col(cNR))
+            act(V("Cd"), V("Cd"), ACT.Relu, bias=1.0, scale=-1.0)
+            act(V("Cd"), V("Cd"), ACT.Identity, bias=1.0, scale=511.0)
+            act(V("Cd", 0, 576, 96), V("cm16", 0, 6), ACT.Identity, scale=0.0)
+        zb = (3, 1)
+        for h in range(2):
+            for k in (2 * h, 2 * h + 1):
+                tt(V("Z", 384 * k, 384 * k + 384), V("Xh"), V("Yh"), ALU.add, off=V("LT", 24 * k, 24 * k + 24))
+                if k == 0:
+                    disc_list(M, C)
+            quant("z%d" % t, 192 * h, "Z", 192 * h, 192)
+            mm(zb[h], "ub", 128, "z%d" % t, 192 * h, 192)
+        for h in range(2):
+            tt(V("sm", 192 * h, 192 * h + 192), PS(zb[h], 0, 192), V("Bm", 0, 192), ALU.add)
+            scan(V("ss", 192 * h, 192 * h + 192), V("Am", 0, 192), V("sm", 192 * h, 192 * h + 192), -BIG, ALU.add, ALU.max)
+        s0, s1 = V("ss", 15, 288, 16), V("ss", 111, 384, 16)
+        tt(V("G"), s1, s0, ALU.is_gt)
+        tt(V("Mx"), s1, s0, ALU.max)
+        tt(V("GJ"), V("G"), V("JJ", 6, 24), ALU.mult)
+        tt(V("hh"), V("Mx", 12, 18), V("Mx", 0, 6), ALU.is_gt)
+        tt(V("AB"), V("GJ"), V("JJ", 0, 18), ALU.max)
+        tt(V("Bh"), V("AB", 12, 18), V("hh"), ALU.mult)
+        idx = V("IDX", 6 * t, 6 * t + 6)
+        tt(idx, V("Bh"), V("AB", 0, 6), ALU.max)
+        cp(V("L96"), idx)
+        ts(V("LH", 0, 6), idx, 4.0, ALU.mult)
+        act(V("wrow"), V("E"), ACT.Copy, off=V("L96"))
+        pick_scales("h%d" % t, "z%d" % t, C, V("L96"))
+        tt(V("wm"), V("E"), V("Bm", 0, M), ALU.add, off=V("L96"))
+        pick_codes("h%d" % t, "z%d" % t, C, V("L96"))
+        rid, pid = topo.addr(nxt)[0], topo.addr(nxt)[1]
+        for pre in ("q", "s"):
+            src = V(pre + "h%d" % t)
+            dst = T[pre + "l%d" % t][:, 0:M]
+            need("g", [src], [])
+            if pre == "q":
+                g.remote_dma(dst.bitcast(dt.uint8), src[0].bitcast(dt.uint8), T.sem["arr%d" % t], T.sem.sent, pid, rid,
+                             topo.mask(core, nxt))
+            else:
+                g.remote_dma(dst, src[0], T.sem["arr%d" % t], T.sem.sent, pid, rid, topo.mask(core, nxt))
+            count["sent"] += len(topo.engines(core, nxt))
+        scan(V("wS"), V("Am", 0, M), V("wm"), -BIG, ALU.add, ALU.max)
+        for e in range(1, 4):
+            ts(V("LH", 6 * e, 6 * e + 6), idx, 4.0, ALU.mult, float(e), ALU.add)
+        act(V("Hp"), V("Z"), ACT.Copy, off=V("LH"))
+        for i in range(6):
+            ts(V("EQ", 96 * i, 112 * i + 16), V("wrow", 0, 16 * i + 16), V("wS", 16 * i + 15, 16 * i + 16), ALU.is_equal)
+        scan(V("ds"), V("Cd"), V("EQ"), 0.0, ALU.mult, ALU.add)
+        if t == 0:
+            quant("e0", 0, "Et", 0, 128)
+        tt(V("zz"), V("ds", 95, 576, 96), V("DUM"), ALU.min)
+        if t == 0:
+            quant("l0", M, "zero", 0, 128)
+        tt(V("w2"), V("zz"), V("wS", 15, M, 16), ALU.max)
+        if t == 0:
+            quant("e0", 128, "Et", 128, 384)
+        for e in range(4):
+            ts(V("LS", 6 * e, 6 * e + 6), V("w2"), 4.0, ALU.mult, float(e - 128), ALU.add)
+        scatter(V("X"), V("LS"), V("Hp"))
+
+    layer(R - 1)
+    for b in range(4):
+        mm(b, "e0", 128 * b, "l%d" % (R - 1), 0, 128)
+        act(V("RL", 96 * b, 96 * b + 96), PS(4 + b, 0, M), ACT.Relu, scale=0.03125)
+    quant("a", 0, "X", 0, C)
+    mm(4, "v0", 0, "a", 0, C)
+    dma("s", T.oc[:, 0:4 * C], T.qa[:, 0:C].bitcast(dt.uint8), [V("qa", 0, C)], [])
+    for t in range(R):
+        tt(V("kd", 6 * t, 6 * t + 6), V("IDX", 6 * t, 6 * t + 6), V("JJ", 0, 6), ALU.subtract)
+    ts(V("kk"), V("kd"), 1.0 / M, ALU.mult)
+    op("v", lambda: g.vector.transpose(T.kT[0:32, :], T.kk[0:32, :]), [V("kk")], [V("kT")])
+    dma("s", T.ok[:], T.kT[0:18, 0:16], [V("kT")], [])
+    add_d(0)
+    quant("a", C, "Y", 0, 128)
+    mm(5, "v0", 0, "a", C, 128)
+    act(V("yo", 0, C), PS(4, 0, C), ACT.Copy)
+    dma("a", T.y[:, 0:C], T.yo[:, 0:C], [V("yo", 0, C)], [])
+    dma("s", T.oc[:, 4 * C:4 * (C + M)], T.qa[:, C:C + M].bitcast(dt.uint8), [V("qa", C, C + M)], [])
+    for k in range(4):
+        dma("sasa"[k], T.osc[4 * k:4 * k + 4, :], T.sa[32 * k:32 * k + 4, 0:C + M], [V("sa")], [])
+    cp(V("yo", C, C + M), PS(5, 0, M))
+    dma("s", T.y[:, C:C + M], T.yo[:, C:C + M], [V("yo", C, C + M)], [])
+    g.wait_ge(T.sem.sent, count["sent"])
+    for sem in sorted(last):
+        if known["g"].get(sem, 0) < last[sem]:
+            g.wait_ge(T.sem[sem], last[sem])

@@ -3,24 +3,24 @@ from concourse.mybir import dt, AluOpType as ALU, ActivationFunctionType as ACT
 C, M, R = 384, 96, 3
 BIG = 2.0 ** 98
 K = 16384.0
-NV = 10
+NV = 9
 TW = [384, 320, 256, 192, 128, 128]
 TO = [0, 384, 704, 960, 1152, 1280]
 MO = [0, 96, 192, 320, 416, 512]
 CODES = "float8_e4m3fn_x4"
 
 SCRATCH = {"ps": ("psum", [128, 4096], "float32")}
-for _n, _w in (("X", 1920), ("Y", 512), ("Xh", 1536), ("Yh", 384), ("Z", 1536), ("Hp", 384), ("ut", 512), ("vt", 512),
+for _n, _w in (("X", 3456), ("Y", 512), ("Xh", 1536), ("Yh", 384), ("Z", 1536), ("Hp", 384), ("ut", 512), ("vt", 512),
                ("MT", 4 * 1408), ("MM", 4 * 640), ("junk", 4416), ("ones", 512), ("blk0", 512), ("blk", 512),
                ("Et", 2048), ("zero", 512), ("cm16", 384), ("Bm", 384), ("Am", 384), ("Rst", 384), ("Cc", 384),
-               ("C4", 288), ("cdv", 576), ("Cd", 576), ("EQ", 576), ("ds", 576), ("drow", 384)):
+               ("C4", 256), ("cdv", 576), ("Cd", 576), ("EQ", 576), ("ds", 576), ("drow", 384)):
     SCRATCH[_n] = ("sbuf", [128, _w], "bfloat16")
-for _n, _w in (("col", 16), ("i16", 24), ("JJ", 24), ("Ctab", 24), ("DUM", 6), ("V16", 48), ("V4", 12), ("kf", 16),
-               ("kb", 16), ("cvals", 384), ("msk", 384), ("Sc", 384), ("Rtab", 24), ("CD", 24), ("CR", 24),
-               ("CRK", 24), ("nst", 96), ("pos", 24), ("pwr", 24), ("pos2", 24), ("pst", 384), ("pl", 24), ("O", 384),
-               ("E", 384), ("Tst", 384), ("sm", 384), ("ss", 384), ("Mx", 18), ("G", 18), ("hh", 6), ("GJ", 18),
-               ("AB", 18), ("Bh", 6), ("IDX", 18), ("wrow", 96), ("wm", 96), ("wS", 96), ("zz", 6), ("w2", 6),
-               ("RL", 384), ("kd", 32), ("kk", 32), ("kT", 32), ("yo", 480)):
+for _n, _w in (("col", 16), ("i16", 24), ("JJ", 24), ("Ctab", 24), ("DUM", 6), ("d0", 24), ("d1", 24), ("V16", 48),
+               ("V4", 12), ("kf", 16), ("kb", 16), ("cvals", 384), ("msk", 384), ("Sc", 384), ("Rtab", 24), ("CD", 24),
+               ("CR", 24), ("CRK", 24), ("nst", 96), ("pos", 24), ("pwr", 24), ("pos2", 24), ("pst", 384), ("pl", 24),
+               ("O", 384), ("E", 384), ("Tst", 384), ("sm", 384), ("ss", 384), ("Mx", 18), ("G", 6), ("IDX", 72),
+               ("wrow", 96), ("wm", 96), ("wS", 96), ("w2", 6), ("RL", 384), ("kd", 32), ("kk", 32), ("kT", 32),
+               ("yo", 480)):
     SCRATCH[_n] = ("sbuf", [128, _w], "float32")
 for _n, _w in (("pi", 2), ("pj", 4), ("uli", 16), ("ki", 16)):
     SCRATCH[_n] = ("sbuf", [128, _w], "int32")
@@ -207,14 +207,20 @@ def rank_program(g, core, T, topo):
     fill(V("MT", 4 * (TO[5] + 16), 4 * 1408), 0.0)
     ts(V("col", cR1, cA1 + 1), V("col", cR, cA + 1), 1.0, ALU.add)
     ts(col(cS16), col(cR), 15.0, ALU.is_equal, 1.0 / K, ALU.max)
-    ts(col(cK16), col(cR), 15.0, ALU.not_equal, K, ALU.mult)
-    ts(col(cS4), col(cA), 3.0, ALU.is_equal, 1.0 / K, ALU.max)
-    ts(V("Bm"), V("cm16"), col(cR), ALU.not_equal, -BIG, ALU.mult)
-    ts(V("Am"), V("cm16"), 0.0, ALU.is_equal, -BIG, ALU.mult)
     ts(V("V16", 0, 16), V("cm16", 0, 16), col(cR1), ALU.is_gt)
     ts(V("V16", 16, 32), V("cm16", 0, 16), col(cR1), ALU.is_equal, K, ALU.mult)
-    ts(col(cT4), col(cT), -128.0, ALU.add)
+    ts(V("Bm"), V("cm16"), col(cR), ALU.not_equal, -BIG, ALU.mult)
     tt(V("V16", 32, 48), V("V16", 0, 16), V("V16", 16, 32), ALU.add)
+    for c in range(16):
+        act(V("Cc", c, 384, 16), V("cm16", 0, 24), ACT.Identity, bias=V("V16", 32 + c, 33 + c), scale=0.0)
+    ts(V("Am"), V("cm16"), 0.0, ALU.is_equal, -BIG, ALU.mult)
+    ts(col(cK16), col(cR), 15.0, ALU.not_equal, K, ALU.mult)
+    ts(col(cS4), col(cA), 3.0, ALU.is_equal, 1.0 / K, ALU.max)
+    ts(col(cT4), col(cT), -128.0, ALU.add)
+    ts(V("Rst"), V("cm16"), 0.0, ALU.not_equal)
+    ts(V("V4", 0, 4), V("cm16", 0, 4), col(cA1), ALU.is_gt)
+    ts(V("V4", 4, 8), V("cm16", 0, 4), col(cA1), ALU.is_equal, K, ALU.mult)
+    ts(V("JJ"), V("i16"), col(cR), ALU.add)
     quant("u0", 0, "ut", 0, 128)
     ts(col(cNR), col(cR), -1.0, ALU.mult)
     pick_codes("ub", "u0", 128, V("ul"))
@@ -228,19 +234,13 @@ def rank_program(g, core, T, topo):
     zeros("MM", 4 * 608, 4 * 640)
     zeros("Rtab", 0, 1)
 
-    def late_constants(part):
-        if part == 0:
-            ts(V("Rst"), V("cm16"), 0.0, ALU.not_equal)
-            ts(V("V4", 0, 4), V("cm16", 0, 4), col(cA1), ALU.is_gt)
-            ts(V("V4", 4, 8), V("cm16", 0, 4), col(cA1), ALU.is_equal, K, ALU.mult)
-            ts(V("JJ"), V("i16"), col(cR), ALU.add)
-            return
+    def late_constants():
         ts(V("Ctab"), V("i16"), col(cR), ALU.subtract, 15.0, ALU.add)
         cp(V("kf", p=(0, 1)), V("ki", p=(0, 1)))
         ts(col(cK16), col(cK16), 1.0, ALU.max)
         ts(col(cS4), col(cS4), 4.0, ALU.mult)
         tt(V("V4", 8, 12), V("V4", 0, 4), V("V4", 4, 8), ALU.add)
-        ts(V("DUM"), V("JJ", 0, 6), 416.0, ALU.add)
+        ts(V("DUM"), V("JJ", 0, 6), 4.0, ALU.mult, 511.0, ALU.add)
         op("g", lambda: g.partition_broadcast(T.kb[:], T.kf[0:1, :], 128), [V("kf")], [V("kb")])
         iota(V("cvals"), [[1, 384]], 32, 0)
         zeros("O", 0, 384)
@@ -272,17 +272,12 @@ def rank_program(g, core, T, topo):
         for b in range(4):
             tt(V("Y", b, 384, 4), PS(bank0 + b, 0, M), V("RL", 96 * b, 96 * b + 96), ALU.add)
 
-    def disc_list(a, b):
-        scan(V("Tst", a, b), V("C4", 0, b - a), V("E", a, b), 0.0, ALU.mult, ALU.add)
-        ts(V("LT", a // 4, b // 4), V("Tst", a + 3, b, 4), col(cS4), ALU.mult, col(cT4), ALU.add)
+    def winners(t):
+        tt(V("kd", 6 * t, 6 * t + 6), V("IDX", 24 * t + 3, 24 * t + 24, 4), V("JJ", 0, 6), ALU.subtract)
 
     for t in range(R):
         quant("a", 256, "X", 256, 128)
         mm(3, "ub", 0, "a", 256, 128)
-        if t == 0:
-            late_constants(0)
-            for c in range(16):
-                act(V("Cc", c, 384, 16), V("cm16", 0, 24), ACT.Identity, bias=V("V16", 32 + c, 33 + c), scale=0.0)
         quant("a", 0, "X", 0, 256)
         mm(1, "ub", 0, "a", 0, C)
         mm(0, "ub", 0, "a", 0, 256)
@@ -292,13 +287,8 @@ def rank_program(g, core, T, topo):
         if t == 1:
             quant("l1", M, "zero", 0, 128)
         if t == 2:
-            quant("l2", M, "zero", 0, 128)
-        scan(V("Sc", 256, C), V("Am", 0, 128), V("msk", 256, C), -BIG, ALU.add, ALU.max)
-        if t == 0:
-            late_constants(1)
-        if t == 2:
             quant("v0", 0, "vt", 0, 128)
-        tt(slot(24, 256, C), V("Sc", 256, C), PS(3, 0, 128), ALU.is_ge)
+        scan(V("Sc", 256, C), V("Am", 0, 128), V("msk", 256, C), -BIG, ALU.add, ALU.max)
         rows = list(range(23, NV, -1))
         done = {}
 
@@ -319,8 +309,16 @@ def rank_program(g, core, T, topo):
             mm(2, "one", 0, "mt", TO[k], TW[k], len(done) == 1, len(done) == 6)
 
         scalar_rows(17)
+        if t == 0:
+            late_constants()
         tt(V("msk", 0, 256), PS(0, 0, 256), V("Bm", 0, 256), ALU.add)
+        tt(slot(24, 256, C), V("Sc", 256, C), PS(3, 0, 128), ALU.is_ge)
         scan(V("Sc", 0, 256), V("Am", 0, 256), V("msk", 0, 256), -BIG, ALU.add, ALU.max)
+        if t == 1:
+            quant("l2", M, "zero", 0, 128)
+        if t == 2:
+            winners(0)
+            winners(1)
         tt(slot(24, 0, 256), V("Sc", 0, 256), PS(0, 0, 256), ALU.is_ge)
         for i in range(NV, 0, -1):
             ts(slot(i), PS(0, 0, 16 * i), pt(i), ALU.is_lt)
@@ -328,9 +326,9 @@ def rank_program(g, core, T, topo):
         if t > 0:
             relu_then_d(t - 1)
         tile_sum(0)
-        tt(V("CD"), V("Ctab"), V("drow", 15, 384, 16), ALU.subtract)
         if t > 0:
             add_d(4)
+        tt(V("CD"), V("Ctab"), V("drow", 15, 384, 16), ALU.subtract)
         quant("a", C, "Y", 0, 128)
         mm(3, "ub", 0, "a", C, 128)
         if t == 0:
@@ -348,59 +346,80 @@ def rank_program(g, core, T, topo):
             for i in range(12 * half, 12 * half + 12):
                 k, e = divmod(i, 4)
                 ts(V("MM", 4 * MO[k] + e, 4 * (MO[k] + M), 4), PS(3, 0, M), pt(i), ALU.is_lt)
-                if i % 12 == 5:
-                    tile_sum(1 + half)
-                    tile_mm(1 + half)
+            if half == 0:
+                tile_sum(1)
+                tile_mm(1)
             quant("mm", 320 * half, "MM", 320 * half, 320 if t == 0 else 288)
             for k in range(3 * half, 3 * half + 3):
                 mm(4, "one", 0, "mm", MO[k], 128, k == 0, k == 5)
-        tile_sum(3)
-        tile_mm(3)
-        tt(V("CR"), V("CD"), V("Rtab"), ALU.subtract)
+        for k in (2, 3):
+            tile_sum(k)
+            tile_mm(k)
         scan(V("nst"), V("Cc", 0, M), PS(4, 0, M), 0.0, ALU.mult, ALU.add)
-        ts(V("CRK"), V("CR"), col(cK16), ALU.mult)
+        tt(V("CR"), V("CD"), V("Rtab"), ALU.subtract)
         for k in range(4):
             act(V("pos", 6 * k, 6 * k + 6), V("nst", 15, M, 16), ACT.Identity, bias=V("kb", k, k + 1), scale=col(cS16))
+        ts(V("CRK"), V("CR"), col(cK16), ALU.mult)
         scan(V("pst"), V("Cc"), PS(2, 0, C), 0.0, ALU.mult, ALU.add)
-        tt(V("pl"), V("pst", 15, C, 16), V("CRK"), ALU.add)
         ts(V("pwr"), V("pos"), float(C), ALU.is_ge, -float(C), ALU.mult)
-        ts(V("Lp"), V("pl"), col(cS16), ALU.mult)
+        tt(V("pl"), V("pst", 15, C, 16), V("CRK"), ALU.add)
         tt(V("pos2"), V("pos"), V("pwr"), ALU.add)
+        ts(V("Lp"), V("pl"), col(cS16), ALU.mult)
         if t == 0:
             for c in range(4):
-                act(V("C4", c, 288, 4), V("cm16", 0, 72), ACT.Identity, bias=V("V4", 8 + c, 9 + c), scale=0.0)
+                act(V("C4", c, 256, 4), V("cm16", 0, 64), ACT.Identity, bias=V("V4", 8 + c, 9 + c), scale=0.0)
         act(V("Xh"), V("X", 0, 1536), ACT.Identity, scale=0.5)
         act(V("Yh"), V("Y", 0, 384), ACT.Identity, scale=0.5)
         cp(V("Lpos"), V("pos2"))
         scatter(V("O"), V("Lp"), V("cvals"))
-        act(V("E", M, C), V("O"), ACT.Copy, off=V("Lpos", 6, 24))
-        gather(V("E", 0, M), V("O"), V("Lpos", 0, 6))
-        disc_list(0, M)
+        act(V("E", 128, C), V("O"), ACT.Copy, off=V("Lpos", 8, 24))
+        gather(V("E", 0, 128), V("O"), V("Lpos", 0, 8))
+        for a, b in ((0, 128), (128, C)):
+            scan(V("Tst", a, b), V("C4", 0, b - a), V("E", a, b), 0.0, ALU.mult, ALU.add)
+        for a, b in ((0, 128), (128, C)):
+            ts(V("LT", a // 4, b // 4), V("Tst", a + 3, b, 4), col(cS4), ALU.mult, col(cT4), ALU.add)
         if t == 0:
             act(V("Cd"), V("cdv"), ACT.Abs, bias=col(cNR))
             act(V("Cd"), V("Cd"), ACT.Relu, bias=1.0, scale=-1.0)
-            act(V("Cd"), V("Cd"), ACT.Identity, bias=1.0, scale=511.0)
+            for i in range(6):
+                seg = V("Cd", 96 * i, 96 * i + 96)
+                act(seg, seg, ACT.Identity, bias=1.0, scale=V("DUM", i, i + 1))
             act(V("Cd", 0, 576, 96), V("cm16", 0, 6), ACT.Identity, scale=0.0)
-        zb = (3, 1)
-        for h in range(2):
-            for k in (2 * h, 2 * h + 1):
-                tt(V("Z", 384 * k, 384 * k + 384), V("Xh"), V("Yh"), ALU.add, off=V("LT", 24 * k, 24 * k + 24))
-                if k == 0:
-                    disc_list(M, C)
+            for e, c in ((0, 288.0), (1, 192.0), (2, 0.0)):
+                act(V("d1", e, 24, 4), V("JJ", 0, 6), ACT.Identity, bias=c)
+            for e in (0, 3):
+                act(V("d0", e, 24, 4), V("JJ", 0, 6), ACT.Identity, bias=float(e // 3), scale=0.0)
+
+        def z(k):
+            tt(V("Z", 384 * k, 384 * k + 384), V("Xh"), V("Yh"), ALU.add, off=V("LT", 24 * k, 24 * k + 24))
+
+        def scores(h, bank):
             quant("z%d" % t, 192 * h, "Z", 192 * h, 192)
-            mm(zb[h], "ub", 128, "z%d" % t, 192 * h, 192)
-        for h in range(2):
-            tt(V("sm", 192 * h, 192 * h + 192), PS(zb[h], 0, 192), V("Bm", 0, 192), ALU.add)
+            mm(bank, "ub", 128, "z%d" % t, 192 * h, 192)
+
+        def masked(h, bank):
+            tt(V("sm", 192 * h, 192 * h + 192), PS(bank, 0, 192), V("Bm", 0, 192), ALU.add)
+
+        def held(h):
             scan(V("ss", 192 * h, 192 * h + 192), V("Am", 0, 192), V("sm", 192 * h, 192 * h + 192), -BIG, ALU.add, ALU.max)
-        s0, s1 = V("ss", 15, 288, 16), V("ss", 111, 384, 16)
-        tt(V("G"), s1, s0, ALU.is_gt)
-        tt(V("Mx"), s1, s0, ALU.max)
-        tt(V("GJ"), V("G"), V("JJ", 6, 24), ALU.mult)
-        tt(V("hh"), V("Mx", 12, 18), V("Mx", 0, 6), ALU.is_gt)
-        tt(V("AB"), V("GJ"), V("JJ", 0, 18), ALU.max)
-        tt(V("Bh"), V("AB", 12, 18), V("hh"), ALU.mult)
-        idx = V("IDX", 6 * t, 6 * t + 6)
-        tt(idx, V("Bh"), V("AB", 0, 6), ALU.max)
+
+        z(0)
+        z(1)
+        z(2)
+        scores(0, 3)
+        z(3)
+        masked(0, 3)
+        scores(1, 1)
+        held(0)
+        masked(1, 1)
+        held(1)
+        tt(V("Mx"), V("ss", 111, 384, 16), V("ss", 15, 288, 16), ALU.max)
+        tt(V("G"), V("ss", 111, 192, 16), V("ss", 15, 96, 16), ALU.is_gt)
+        tt(V("d0", 1, 24, 4), V("ss", 303, 384, 16), V("ss", 207, 288, 16), ALU.is_gt)
+        tt(V("d0", 2, 24, 4), V("Mx", 12, 18), V("Mx", 0, 6), ALU.is_gt)
+        tt(V("d1", 3, 24, 4), V("G"), V("JJ", 6, 12), ALU.mult)
+        scan(V("IDX", 24 * t, 24 * t + 24), V("d0"), V("d1"), 0.0, ALU.mult, ALU.max)
+        idx = V("IDX", 24 * t + 3, 24 * t + 24, 4)
         cp(V("L96"), idx)
         ts(V("LH", 0, 6), idx, 4.0, ALU.mult)
         act(V("wrow"), V("E"), ACT.Copy, off=V("L96"))
@@ -419,34 +438,34 @@ def rank_program(g, core, T, topo):
                 g.remote_dma(dst, src[0], T.sem["arr%d" % t], T.sem.sent, pid, rid, topo.mask(core, nxt))
             count["sent"] += len(topo.engines(core, nxt))
         scan(V("wS"), V("Am", 0, M), V("wm"), -BIG, ALU.add, ALU.max)
-        for e in range(1, 4):
-            ts(V("LH", 6 * e, 6 * e + 6), idx, 4.0, ALU.mult, float(e), ALU.add)
-        act(V("Hp"), V("Z"), ACT.Copy, off=V("LH"))
+        ts(V("LH", 6, 12), idx, 4.0, ALU.mult, 1.0, ALU.add)
         for i in range(6):
             ts(V("EQ", 96 * i, 112 * i + 16), V("wrow", 0, 16 * i + 16), V("wS", 16 * i + 15, 16 * i + 16), ALU.is_equal)
-        scan(V("ds"), V("Cd"), V("EQ"), 0.0, ALU.mult, ALU.add)
+        for e in range(2, 4):
+            ts(V("LH", 6 * e, 6 * e + 6), idx, 4.0, ALU.mult, float(e), ALU.add)
+        act(V("Hp"), V("Z"), ACT.Copy, off=V("LH"))
+        scan(V("ds"), V("Cd"), V("EQ"), 0.0, ALU.mult, ALU.max)
         if t == 0:
-            quant("e0", 0, "Et", 0, 128)
-        tt(V("zz"), V("ds", 95, 576, 96), V("DUM"), ALU.min)
+            quant("e0", 0, "Et", 0, 256)
+        tt(V("w2"), V("ds", 95, 576, 96), V("wS", 15, M, 16), ALU.max)
         if t == 0:
-            quant("l0", M, "zero", 0, 128)
-        tt(V("w2"), V("zz"), V("wS", 15, M, 16), ALU.max)
-        if t == 0:
-            quant("e0", 128, "Et", 128, 384)
+            quant("e0", 256, "Et", 256, 256)
         for e in range(4):
             ts(V("LS", 6 * e, 6 * e + 6), V("w2"), 4.0, ALU.mult, float(e - 128), ALU.add)
+        if t == 0:
+            quant("l0", M, "zero", 0, 128)
+        if t == R - 1:
+            winners(t)
         scatter(V("X"), V("LS"), V("Hp"))
 
     layer(R - 1)
     for b in range(4):
         mm(b, "e0", 128 * b, "l%d" % (R - 1), 0, 128)
         act(V("RL", 96 * b, 96 * b + 96), PS(4 + b, 0, M), ACT.Relu, scale=0.03125)
+    ts(V("kk"), V("kd"), 1.0 / M, ALU.mult)
     quant("a", 0, "X", 0, C)
     mm(4, "v0", 0, "a", 0, C)
     dma("s", T.oc[:, 0:4 * C], T.qa[:, 0:C].bitcast(dt.uint8), [V("qa", 0, C)], [])
-    for t in range(R):
-        tt(V("kd", 6 * t, 6 * t + 6), V("IDX", 6 * t, 6 * t + 6), V("JJ", 0, 6), ALU.subtract)
-    ts(V("kk"), V("kd"), 1.0 / M, ALU.mult)
     op("v", lambda: g.vector.transpose(T.kT[0:32, :], T.kk[0:32, :]), [V("kk")], [V("kT")])
     dma("s", T.ok[:], T.kT[0:18, 0:16], [V("kT")], [])
     add_d(0)

from concourse.mybir import dt, AluOpType as ALU, ActivationFunctionType as ACT

C, M, R = 384, 96, 3
BIG = 2.0 ** 98
K = 16384.0
NV = 9
TW = [384, 320, 256, 192, 128, 128]
TO = [0, 384, 704, 960, 1152, 1280]
MO = [0, 96, 192, 320, 416, 512]
CODES = "float8_e4m3fn_x4"

SCRATCH = {"ps": ("psum", [128, 4096], "float32")}
for _n, _w in (("X", 3456), ("Y", 512), ("Xh", 1536), ("Yh", 384), ("Z", 1536), ("Hp", 384), ("ut", 512), ("vt", 512),
               ("MT", 4 * 1408), ("MM", 4 * 640), ("junk", 4416), ("ones", 512), ("blk0", 512), ("blk", 512),
               ("Et", 2048), ("zero", 512), ("cm16", 384), ("Bm", 384), ("Am", 384), ("Rst", 384), ("Cc", 384),
               ("C4", 256), ("cdv", 576), ("Cd", 576), ("EQ", 576), ("ds", 576), ("drow", 384)):
    SCRATCH[_n] = ("sbuf", [128, _w], "bfloat16")
for _n, _w in (("col", 16), ("i16", 24), ("JJ", 24), ("Ctab", 24), ("DUM", 6), ("d0", 24), ("d1", 24), ("V16", 48),
               ("V4", 12), ("kf", 16), ("kb", 16), ("cvals", 384), ("msk", 384), ("Sc", 384), ("Rtab", 24), ("CD", 24),
               ("CR", 24), ("CRK", 24), ("nst", 96), ("pos", 24), ("pwr", 24), ("pos2", 24), ("pst", 384), ("pl", 24),
               ("O", 384), ("E", 384), ("Tst", 384), ("sm", 384), ("ss", 384), ("Mx", 18), ("G", 6), ("IDX", 72),
               ("wrow", 96), ("wm", 96), ("wS", 96), ("w2", 6), ("RL", 384), ("kd", 32), ("kk", 32), ("kT", 32),
               ("yo", 480)):
    SCRATCH[_n] = ("sbuf", [128, _w], "float32")
for _n, _w in (("pi", 2), ("pj", 4), ("uli", 16), ("ki", 16)):
    SCRATCH[_n] = ("sbuf", [128, _w], "int32")
for _n, _w in (("ul", 16), ("Lp", 24), ("Lpos", 24), ("LT", 96), ("L96", 6), ("LH", 24), ("LS", 24)):
    SCRATCH[_n] = ("sbuf", [128, _w], "uint16")
for _n, _w in ([("u0", 128), ("ub", 256), ("v0", 128), ("w0", 512), ("e0", 512), ("one", 128), ("a", 512),
                ("mt", 1408), ("mm", 640)] + [("z%d" % _t, 384) for _t in range(R)]
               + [("h%d" % _t, 96) for _t in range(R)] + [("l%d" % _t, 224) for _t in range(R)]):
    SCRATCH["q" + _n] = ("sbuf", [128, _w], CODES)
    SCRATCH["s" + _n] = ("sbuf", [128, _w], "uint8")

SEMAPHORES = ["sv", "sa", "st", "sg", "sent", "arr0", "arr1", "arr2"] + ["d%d" % _i for _i in range(24)]


def rank_program(g, core, T, topo):
    rank = T.rank_of(core)
    if rank is None:
        return
    n = len(T.cores)
    nxt, prv = T.cores[(rank + 1) % n], T.cores[(rank - 1) % n]
    Q = {"v": g.vector, "a": g.scalar, "t": g.tensor, "g": g, "s": g.sync}
    SEM = {"v": "sv", "a": "sa", "t": "st", "g": "sg"}
    count = {"v": 0, "a": 0, "t": 0, "g": 0, "d": 0, "sent": 0, "all": 0}
    known = {q: {} for q in Q}
    hist = {}
    last = {}

    def V(name, a=0, b=None, s=1, p=None):
        if b is None:
            b = SCRATCH[name][1][1]
        m = 0
        if s == 1:
            m = ((1 << (b - a)) - 1) << a
        else:
            for i in range(a, b, s):
                m |= 1 << i
        rows = slice(0, 128) if p is None else slice(p[0], p[1])
        ap = T[name][rows, a:b] if s == 1 else T[name][rows, a:b:s]
        return (ap, name, m)

    def PS(bank, a, b):
        return (T.ps[:, 512 * bank + a:512 * bank + b], "ps%d" % bank, 1)

    def need(q, reads, writes):
        deps = []
        for vs, w in ((reads, False), (writes, True)):
            for x in vs:
                bank = x[1].startswith("ps")
                for (m, w2, tok, q2) in hist.get(x[1], []):
                    if m & x[2] and (w or w2 or (bank and q2 != q)) and not (q == "t" and q2 == "t"):
                        deps.append(tok)
        deps.sort(key=lambda k: -k[3])
        for sem, val, clock, _ in deps:
            if known[q].get(sem, 0) < val:
                Q[q].wait_ge(T.sem[sem], val)
                known[q][sem] = val
                for s2, v2 in clock.items():
                    if known[q].get(s2, 0) < v2:
                        known[q][s2] = v2

    def note(q, sem, val, reads, writes):
        count["all"] += 1
        tok = (sem, val, dict(known[q]) if q in known else {}, count["all"])
        last[sem] = val
        for vs, w in ((reads, False), (writes, True)):
            for x in vs:
                h = hist.setdefault(x[1], [])
                if w:
                    h[:] = [e for e in h if e[0] & ~x[2]]
                h.append((x[2], w, tok, q))

    def op(q, fn, reads, writes):
        reads = [x for x in reads if isinstance(x, tuple)]
        need(q, reads, writes)
        count[q] += 1
        fn().then_inc(T.sem[SEM[q]], 1)
        note(q, SEM[q], count[q], reads, writes)

    def dma(q, out, in_, reads, writes):
        need(q, reads, writes)
        sem = "d%d" % count["d"]
        count["d"] += 1
        Q[q].dma_start(out, in_).then_inc(T.sem[sem], 16)
        note(q, sem, 16, reads, writes)

    def A(x):
        return x[0] if isinstance(x, tuple) else x

    def tt(out, a, b, o, off=None):
        i0 = a[0] if off is None else a[0].indirect(off[0])
        op("v", lambda: g.vector.tensor_tensor(out[0], i0, b[0], o), [a, b, off], [out])

    def ts(out, a, s1, o0, s2=None, o1=None):
        if o1 is None:
            op("v", lambda: g.vector.tensor_scalar(out[0], a[0], A(s1), None, o0), [a, s1], [out])
        else:
            op("v", lambda: g.vector.tensor_scalar(out[0], a[0], A(s1), A(s2), o0, o1), [a, s1, s2], [out])

    def cp(out, a):
        op("v", lambda: g.vector.tensor_copy(out[0], a[0]), [a], [out])

    def gather(out, win, off):
        op("v", lambda: g.vector.tensor_copy(out[0], win[0].indirect(off[0])), [win, off], [out])

    def scatter(win, off, a):
        op("v", lambda: g.vector.tensor_copy(win[0].indirect(off[0]), a[0]), [a, off], [win])

    def scan(out, d0, d1, init, o0, o1):
        op("v", lambda: g.vector.tensor_tensor_scan(out[0], d0[0], d1[0], init, o0, o1), [d0, d1], [out])

    def fill(out, c):
        op("v", lambda: g.vector.memset(out[0], c), [], [out])

    def act(out, a, f, bias=None, scale=None, acc=None, off=None):
        kw = {}
        if bias is not None:
            kw["bias"] = A(bias)
        if scale is not None:
            kw["scale"] = A(scale)
        if acc is not None:
            kw["accum_out"] = acc[0]
        i0 = a[0] if off is None else a[0].indirect(off[0])
        op("a", lambda: g.scalar.activation(out[0], i0, f, **kw), [a, bias, scale, off],
           [out] + ([acc] if acc is not None else []))

    def quant(name, c0, tile, t0, cols):
        o, s, i = V("q" + name, c0, c0 + cols), V("s" + name, c0, c0 + cols), V(tile, 4 * t0, 4 * (t0 + cols))
        op("v", lambda: g.vector.quantize_mx(o[0], s[0], i[0]), [i], [o, s])

    def mm(bank, w, w0, x, x0, cols, start=True, stop=True):
        o = PS(bank, 0, cols)
        a, sa = V("q" + w, w0, w0 + 128), V("s" + w, w0, w0 + 128)
        b, sb = V("q" + x, x0, x0 + cols), V("s" + x, x0, x0 + cols)
        op("t", lambda: g.tensor.matmul_mx(o[0], a[0], sa[0], b[0], sb[0], start, stop), [a, sa, b, sb], [o])

    def pick_codes(dst, src, width, off):
        o, w = V("q" + dst), V("q" + src, 0, width)
        op("v", lambda: g.vector.tensor_copy(o[0].bitcast(dt.uint32), w[0].bitcast(dt.uint32).indirect(off[0])),
           [w, off], [o])

    def pick_scales(dst, src, width, off):
        act(V("s" + dst), V("s" + src, 0, width), ACT.Copy, off=off)

    def iota(out, pattern, base, cm, whole=False):
        if whole:
            op("g", lambda: g.iota(out[0], pattern, base, cm), [], [out])
        else:
            op("g", lambda: g.iota(out[0], pattern, base, cm, allow_small_or_imprecise_dtypes=True), [], [out])

    def zeros(name, a, b):
        iota(V(name, a, b), [[0, b - a]], 0, 0)

    def select(out, a, pattern, cmp, base, cm):
        op("g", lambda: g.affine_select(out[0], a[0], pattern, cmp, 0.0, base, cm), [a], [out])

    def col(i):
        return V("col", i, i + 1)

    eng_in = len(topo.engines(prv, core))
    for t in range(R):
        note("remote", "arr%d" % t, 2 * eng_in, [], [V("ql%d" % t, 0, M), V("sl%d" % t, 0, M)])

    dma("a", V("ut")[0], T.u[:], [], [V("ut")])
    dma("s", V("X", 1024, 1536)[0], T.x[:, 1024:1536], [], [V("X", 1024, 1536)])
    dma("s", V("X", 0, 1024)[0], T.x[:, 0:1024], [], [V("X", 0, 1024)])
    dma("s", V("Y", 0, 384)[0], T.m[:], [V("X", 1024, 1536)], [V("Y", 0, 384)])
    dma("s", V("ki", p=(0, 1))[0], T.kap[:], [], [V("ki")])
    dma("s", T.qw0[:].bitcast(dt.uint8), T.wc[:], [V("Y", 0, 384)], [V("qw0")])
    dma("s", T.sw0[:], T.ws[:], [], [V("sw0")])
    dma("s", V("vt")[0], T.v[:], [], [V("vt")])

    cR, cA, cT, cR1, cA1, cS16, cK16, cS4, cT4, cNR = range(10)
    iota(V("pi"), [[0, 2]], 0, 1, whole=True)
    iota(V("uli", 0, 8), [[16, 8]], 0, 0, whole=True)
    iota(V("cm16"), [[0, 24], [1, 16]], 0, 0)
    iota(V("i16"), [[16, 24]], 0, 0)
    fill(V("uli", 8, 16), 1)
    fill(V("ones"), 1.0)
    ts(V("pj", 0, 1), V("pi", 0, 1), 15, ALU.bitwise_and)
    ts(V("pj", 1, 2), V("pi", 0, 1), 2, ALU.logical_shift_right, 3, ALU.bitwise_and)
    ts(V("pj", 2, 3), V("pi", 0, 1), 3, ALU.bitwise_and)
    cp(V("ul"), V("uli"))
    cp(V("col", 0, 3), V("pj", 0, 3))
    fill(V("MT", 4 * (TO[5] + 16), 4 * 1408), 0.0)
    ts(V("col", cR1, cA1 + 1), V("col", cR, cA + 1), 1.0, ALU.add)
    ts(col(cS16), col(cR), 15.0, ALU.is_equal, 1.0 / K, ALU.max)
    ts(V("V16", 0, 16), V("cm16", 0, 16), col(cR1), ALU.is_gt)
    ts(V("V16", 16, 32), V("cm16", 0, 16), col(cR1), ALU.is_equal, K, ALU.mult)
    ts(V("Bm"), V("cm16"), col(cR), ALU.not_equal, -BIG, ALU.mult)
    tt(V("V16", 32, 48), V("V16", 0, 16), V("V16", 16, 32), ALU.add)
    for c in range(16):
        act(V("Cc", c, 384, 16), V("cm16", 0, 24), ACT.Identity, bias=V("V16", 32 + c, 33 + c), scale=0.0)
    ts(V("Am"), V("cm16"), 0.0, ALU.is_equal, -BIG, ALU.mult)
    ts(col(cK16), col(cR), 15.0, ALU.not_equal, K, ALU.mult)
    ts(col(cS4), col(cA), 3.0, ALU.is_equal, 1.0 / K, ALU.max)
    ts(col(cT4), col(cT), -128.0, ALU.add)
    ts(V("Rst"), V("cm16"), 0.0, ALU.not_equal)
    ts(V("V4", 0, 4), V("cm16", 0, 4), col(cA1), ALU.is_gt)
    ts(V("V4", 4, 8), V("cm16", 0, 4), col(cA1), ALU.is_equal, K, ALU.mult)
    ts(V("JJ"), V("i16"), col(cR), ALU.add)
    quant("u0", 0, "ut", 0, 128)
    ts(col(cNR), col(cR), -1.0, ALU.mult)
    pick_codes("ub", "u0", 128, V("ul"))
    pick_scales("ub", "u0", 128, V("ul"))
    for a in range(5):
        zeros("MT", 4 * (TO[a] + TW[a] - 48), 4 * (TO[a] + TW[a]))
    zeros("Y", 384, 512)
    select(V("blk0"), V("ones"), [[-16, 8], [0, 64]], ALU.is_ge, 0, 1)
    select(V("blk"), V("blk0"), [[16, 8], [0, 64]], ALU.is_ge, 15, -1)
    zeros("MM", 4 * 288, 4 * 320)
    zeros("MM", 4 * 608, 4 * 640)
    zeros("Rtab", 0, 1)

    def late_constants():
        ts(V("Ctab"), V("i16"), col(cR), ALU.subtract, 15.0, ALU.add)
        cp(V("kf", p=(0, 1)), V("ki", p=(0, 1)))
        ts(col(cK16), col(cK16), 1.0, ALU.max)
        ts(col(cS4), col(cS4), 4.0, ALU.mult)
        tt(V("V4", 8, 12), V("V4", 0, 4), V("V4", 4, 8), ALU.add)
        ts(V("DUM"), V("JJ", 0, 6), 4.0, ALU.mult, 511.0, ALU.add)
        op("g", lambda: g.partition_broadcast(T.kb[:], T.kf[0:1, :], 128), [V("kf")], [V("kb")])
        iota(V("cvals"), [[1, 384]], 32, 0)
        zeros("O", 0, 384)
        iota(V("cdv"), [[-16, 6], [1, 96]], 0, 0)
        zeros("EQ", 0, 576)
        zeros("zero", 0, 512)
        zeros("kd", 0, 32)
        for b in range(4):
            select(V("Et", 512 * b, 512 * b + 512), V("ones"), [[1, 512]], ALU.is_equal, -b, -4)

    def slot(i, a=0, b=None):
        k, e = divmod(24 - i, 4)
        b = 16 * i if b is None else b
        return V("MT", 4 * (TO[k] + a) + e, 4 * (TO[k] + b), 4)

    def pt(i):
        return V("Sc", 16 * i + 15, 16 * i + 16)

    def layer(t):
        for b in range(4):
            mm(4 + b, "w0", 128 * b, "l%d" % t, 0, 128)

    def relu_then_d(t):
        for b in range(4):
            ts(V("RL", 96 * b, 96 * b + 96), PS(4 + b, 0, M), 0.0, ALU.max, 0.03125, ALU.mult)
            mm(4 + b, "e0", 128 * b, "l%d" % t, 0, 128)

    def add_d(bank0):
        for b in range(4):
            tt(V("Y", b, 384, 4), PS(bank0 + b, 0, M), V("RL", 96 * b, 96 * b + 96), ALU.add)

    def winners(t):
        tt(V("kd", 6 * t, 6 * t + 6), V("IDX", 24 * t + 3, 24 * t + 24, 4), V("JJ", 0, 6), ALU.subtract)

    for t in range(R):
        quant("a", 256, "X", 256, 128)
        mm(3, "ub", 0, "a", 256, 128)
        quant("a", 0, "X", 0, 256)
        mm(1, "ub", 0, "a", 0, C)
        mm(0, "ub", 0, "a", 0, 256)
        if t > 0:
            layer(t - 1)
        tt(V("msk", 256, C), PS(3, 0, 128), V("Bm", 0, 128), ALU.add)
        if t == 1:
            quant("l1", M, "zero", 0, 128)
        if t == 2:
            quant("v0", 0, "vt", 0, 128)
        scan(V("Sc", 256, C), V("Am", 0, 128), V("msk", 256, C), -BIG, ALU.add, ALU.max)
        rows = list(range(23, NV, -1))
        done = {}

        def scalar_rows(upto):
            while rows and rows[0] >= upto:
                two = rows[:2]
                del rows[:2]
                for i in two:
                    act(slot(i), PS(1, 0, 16 * i), ACT.Sign, bias=pt(i), scale=-1.0)
                for i in two:
                    act(slot(i), slot(i), ACT.Relu, acc=V("Rtab", i, i + 1))

        def tile_sum(k, cols=None):
            quant("mt", TO[k], "MT", TO[k], TW[k] if cols is None else cols)

        def tile_mm(k):
            done[k] = True
            mm(2, "one", 0, "mt", TO[k], TW[k], len(done) == 1, len(done) == 6)

        scalar_rows(17)
        if t == 0:
            late_constants()
        tt(V("msk", 0, 256), PS(0, 0, 256), V("Bm", 0, 256), ALU.add)
        tt(slot(24, 256, C), V("Sc", 256, C), PS(3, 0, 128), ALU.is_ge)
        scan(V("Sc", 0, 256), V("Am", 0, 256), V("msk", 0, 256), -BIG, ALU.add, ALU.max)
        if t == 1:
            quant("l2", M, "zero", 0, 128)
        if t == 2:
            winners(0)
            winners(1)
        tt(slot(24, 0, 256), V("Sc", 0, 256), PS(0, 0, 256), ALU.is_ge)
        for i in range(NV, 0, -1):
            ts(slot(i), PS(0, 0, 16 * i), pt(i), ALU.is_lt)
        scan(V("drow"), V("Rst"), slot(24, 0, C), 0.0, ALU.mult, ALU.add)
        if t > 0:
            relu_then_d(t - 1)
        tile_sum(0)
        if t > 0:
            add_d(4)
        tt(V("CD"), V("Ctab"), V("drow", 15, 384, 16), ALU.subtract)
        quant("a", C, "Y", 0, 128)
        mm(3, "ub", 0, "a", C, 128)
        if t == 0:
            quant("one", 0, "blk", 0, 128)
        tile_sum(4, 256 if t == 0 else 192)
        tile_mm(0)
        tile_mm(4)
        tile_mm(5)
        scalar_rows(1)
        off = 0
        for i in range(NV, 0, -1):
            act(V("junk", off, off + 16 * i), slot(i), ACT.Identity, acc=V("Rtab", i, i + 1))
            off += 16 * i
        for half in range(2):
            for i in range(12 * half, 12 * half + 12):
                k, e = divmod(i, 4)
                ts(V("MM", 4 * MO[k] + e, 4 * (MO[k] + M), 4), PS(3, 0, M), pt(i), ALU.is_lt)
            if half == 0:
                tile_sum(1)
                tile_mm(1)
            quant("mm", 320 * half, "MM", 320 * half, 320 if t == 0 else 288)
            for k in range(3 * half, 3 * half + 3):
                mm(4, "one", 0, "mm", MO[k], 128, k == 0, k == 5)
        for k in (2, 3):
            tile_sum(k)
            tile_mm(k)
        scan(V("nst"), V("Cc", 0, M), PS(4, 0, M), 0.0, ALU.mult, ALU.add)
        tt(V("CR"), V("CD"), V("Rtab"), ALU.subtract)
        for k in range(4):
            act(V("pos", 6 * k, 6 * k + 6), V("nst", 15, M, 16), ACT.Identity, bias=V("kb", k, k + 1), scale=col(cS16))
        ts(V("CRK"), V("CR"), col(cK16), ALU.mult)
        scan(V("pst"), V("Cc"), PS(2, 0, C), 0.0, ALU.mult, ALU.add)
        ts(V("pwr"), V("pos"), float(C), ALU.is_ge, -float(C), ALU.mult)
        tt(V("pl"), V("pst", 15, C, 16), V("CRK"), ALU.add)
        tt(V("pos2"), V("pos"), V("pwr"), ALU.add)
        ts(V("Lp"), V("pl"), col(cS16), ALU.mult)
        if t == 0:
            for c in range(4):
                act(V("C4", c, 256, 4), V("cm16", 0, 64), ACT.Identity, bias=V("V4", 8 + c, 9 + c), scale=0.0)
        act(V("Xh"), V("X", 0, 1536), ACT.Identity, scale=0.5)
        act(V("Yh"), V("Y", 0, 384), ACT.Identity, scale=0.5)
        cp(V("Lpos"), V("pos2"))
        scatter(V("O"), V("Lp"), V("cvals"))
        act(V("E", 128, C), V("O"), ACT.Copy, off=V("Lpos", 8, 24))
        gather(V("E", 0, 128), V("O"), V("Lpos", 0, 8))
        for a, b in ((0, 128), (128, C)):
            scan(V("Tst", a, b), V("C4", 0, b - a), V("E", a, b), 0.0, ALU.mult, ALU.add)
        for a, b in ((0, 128), (128, C)):
            ts(V("LT", a // 4, b // 4), V("Tst", a + 3, b, 4), col(cS4), ALU.mult, col(cT4), ALU.add)
        if t == 0:
            act(V("Cd"), V("cdv"), ACT.Abs, bias=col(cNR))
            act(V("Cd"), V("Cd"), ACT.Relu, bias=1.0, scale=-1.0)
            for i in range(6):
                seg = V("Cd", 96 * i, 96 * i + 96)
                act(seg, seg, ACT.Identity, bias=1.0, scale=V("DUM", i, i + 1))
            act(V("Cd", 0, 576, 96), V("cm16", 0, 6), ACT.Identity, scale=0.0)
            for e, c in ((0, 288.0), (1, 192.0), (2, 0.0)):
                act(V("d1", e, 24, 4), V("JJ", 0, 6), ACT.Identity, bias=c)
            for e in (0, 3):
                act(V("d0", e, 24, 4), V("JJ", 0, 6), ACT.Identity, bias=float(e // 3), scale=0.0)

        def z(k):
            tt(V("Z", 384 * k, 384 * k + 384), V("Xh"), V("Yh"), ALU.add, off=V("LT", 24 * k, 24 * k + 24))

        def scores(h, bank):
            quant("z%d" % t, 192 * h, "Z", 192 * h, 192)
            mm(bank, "ub", 128, "z%d" % t, 192 * h, 192)

        def masked(h, bank):
            tt(V("sm", 192 * h, 192 * h + 192), PS(bank, 0, 192), V("Bm", 0, 192), ALU.add)

        def held(h):
            scan(V("ss", 192 * h, 192 * h + 192), V("Am", 0, 192), V("sm", 192 * h, 192 * h + 192), -BIG, ALU.add, ALU.max)

        z(0)
        z(1)
        z(2)
        scores(0, 3)
        z(3)
        masked(0, 3)
        scores(1, 1)
        held(0)
        masked(1, 1)
        held(1)
        tt(V("Mx"), V("ss", 111, 384, 16), V("ss", 15, 288, 16), ALU.max)
        tt(V("G"), V("ss", 111, 192, 16), V("ss", 15, 96, 16), ALU.is_gt)
        tt(V("d0", 1, 24, 4), V("ss", 303, 384, 16), V("ss", 207, 288, 16), ALU.is_gt)
        tt(V("d0", 2, 24, 4), V("Mx", 12, 18), V("Mx", 0, 6), ALU.is_gt)
        tt(V("d1", 3, 24, 4), V("G"), V("JJ", 6, 12), ALU.mult)
        scan(V("IDX", 24 * t, 24 * t + 24), V("d0"), V("d1"), 0.0, ALU.mult, ALU.max)
        idx = V("IDX", 24 * t + 3, 24 * t + 24, 4)
        cp(V("L96"), idx)
        ts(V("LH", 0, 6), idx, 4.0, ALU.mult)
        act(V("wrow"), V("E"), ACT.Copy, off=V("L96"))
        pick_scales("h%d" % t, "z%d" % t, C, V("L96"))
        tt(V("wm"), V("E"), V("Bm", 0, M), ALU.add, off=V("L96"))
        pick_codes("h%d" % t, "z%d" % t, C, V("L96"))
        rid, pid = topo.addr(nxt)[0], topo.addr(nxt)[1]
        for pre in ("q", "s"):
            src = V(pre + "h%d" % t)
            dst = T[pre + "l%d" % t][:, 0:M]
            need("g", [src], [])
            if pre == "q":
                g.remote_dma(dst.bitcast(dt.uint8), src[0].bitcast(dt.uint8), T.sem["arr%d" % t], T.sem.sent, pid, rid,
                             topo.mask(core, nxt))
            else:
                g.remote_dma(dst, src[0], T.sem["arr%d" % t], T.sem.sent, pid, rid, topo.mask(core, nxt))
            count["sent"] += len(topo.engines(core, nxt))
        scan(V("wS"), V("Am", 0, M), V("wm"), -BIG, ALU.add, ALU.max)
        ts(V("LH", 6, 12), idx, 4.0, ALU.mult, 1.0, ALU.add)
        for i in range(6):
            ts(V("EQ", 96 * i, 112 * i + 16), V("wrow", 0, 16 * i + 16), V("wS", 16 * i + 15, 16 * i + 16), ALU.is_equal)
        for e in range(2, 4):
            ts(V("LH", 6 * e, 6 * e + 6), idx, 4.0, ALU.mult, float(e), ALU.add)
        act(V("Hp"), V("Z"), ACT.Copy, off=V("LH"))
        scan(V("ds"), V("Cd"), V("EQ"), 0.0, ALU.mult, ALU.max)
        if t == 0:
            quant("e0", 0, "Et", 0, 256)
        tt(V("w2"), V("ds", 95, 576, 96), V("wS", 15, M, 16), ALU.max)
        if t == 0:
            quant("e0", 256, "Et", 256, 256)
        for e in range(4):
            ts(V("LS", 6 * e, 6 * e + 6), V("w2"), 4.0, ALU.mult, float(e - 128), ALU.add)
        if t == 0:
            quant("l0", M, "zero", 0, 128)
        if t == R - 1:
            winners(t)
        scatter(V("X"), V("LS"), V("Hp"))

    layer(R - 1)
    for b in range(4):
        mm(b, "e0", 128 * b, "l%d" % (R - 1), 0, 128)
        act(V("RL", 96 * b, 96 * b + 96), PS(4 + b, 0, M), ACT.Relu, scale=0.03125)
    ts(V("kk"), V("kd"), 1.0 / M, ALU.mult)
    quant("a", 0, "X", 0, C)
    mm(4, "v0", 0, "a", 0, C)
    dma("s", T.oc[:, 0:4 * C], T.qa[:, 0:C].bitcast(dt.uint8), [V("qa", 0, C)], [])
    op("v", lambda: g.vector.transpose(T.kT[0:32, :], T.kk[0:32, :]), [V("kk")], [V("kT")])
    dma("s", T.ok[:], T.kT[0:18, 0:16], [V("kT")], [])
    add_d(0)
    quant("a", C, "Y", 0, 128)
    mm(5, "v0", 0, "a", C, 128)
    act(V("yo", 0, C), PS(4, 0, C), ACT.Copy)
    dma("a", T.y[:, 0:C], T.yo[:, 0:C], [V("yo", 0, C)], [])
    dma("s", T.oc[:, 4 * C:4 * (C + M)], T.qa[:, C:C + M].bitcast(dt.uint8), [V("qa", C, C + M)], [])
    for k in range(4):
        dma("sasa"[k], T.osc[4 * k:4 * k + 4, :], T.sa[32 * k:32 * k + 4, 0:C + M], [V("sa")], [])
    cp(V("yo", C, C + M), PS(5, 0, M))
    dma("s", T.y[:, C:C + M], T.yo[:, C:C + M], [V("yo", C, C + M)], [])
    g.wait_ge(T.sem.sent, count["sent"])
    for sem in sorted(last):
        if known["g"].get(sem, 0) < last[sem]:
            g.wait_ge(T.sem[sem], last[sem])
